import numpy as np
import ml_dtypes


def mxq(x, axis, fmt="e4m3"):
    dtype, down = {"e4m3": (ml_dtypes.float8_e4m3fn, 7), "e5m2": (ml_dtypes.float8_e5m2, 14)}[fmt]
    v = np.moveaxis(np.asarray(x, np.float32).astype(ml_dtypes.bfloat16).astype(np.float64), axis, -1)
    blocks = v.reshape(v.shape[:-1] + (-1, 32))
    amax = np.abs(blocks).max(-1, keepdims=True)
    byte = np.maximum(np.where(amax > 0, np.frexp(amax)[1] - 1 + 127, 0) - down, 1)
    scale = np.exp2(byte - 127.0)
    codes = (blocks / scale).astype(np.float32).astype(dtype).astype(np.float64)
    return np.moveaxis((codes * scale).reshape(v.shape), -1, axis)


WIDE = False


def mx_kscale(k):
    if not WIDE:
        return np.ones(k)
    levels = np.array([10, -10, 5, -5, 0])
    if k % 512:
        return np.exp2(np.random.permutation(np.resize(levels, k // 32))).repeat(32)
    a = np.empty((k // 512, 16))
    for p in range(k // 512):
        a[p, :8] = np.random.permutation(np.resize(levels, 8))
        for g in range(8):
            far = levels[np.abs(levels - a[p, g]) >= 10]
            a[p, g + 8] = far[np.random.randint(len(far))]
    return np.exp2(a.ravel()).repeat(32)


BF16 = ml_dtypes.bfloat16


def bf(x):
    return np.asarray(x, np.float32).astype(BF16)


def f64(x):
    return np.asarray(x).astype(np.float64)

def planes(Y):
    n, m = Y.shape
    b = f64(bf(Y)).reshape(n // 32, 32, m)
    amax = np.abs(b).max(1)
    byte = np.clip(np.where(amax > 0, np.frexp(amax)[1] - 1 + 127 - 7, 1), 1, 254)
    codes = (b * np.exp2(127.0 - byte)[:, None, :]).reshape(n, m).astype(np.float32).astype(ml_dtypes.float8_e4m3fn).view(np.uint8)
    words = codes.reshape(n // 512, 128, 4, m).transpose(0, 1, 3, 2)
    return np.ascontiguousarray(words), np.ascontiguousarray(byte.astype(np.uint8).reshape(n // 512, 16, m))


R, I, J = 1024, 512, 512


def first_order_density(phi, chi, f):
    cq = mxq(chi * f[None, :], 1, "e4m3")
    pq = mxq(phi, 1, "e4m3")
    a = cq @ pq.T
    return a + a.T


def setup_inputs():
    s, t = mx_kscale(I), mx_kscale(R)
    c = 1.0 / np.sqrt(np.sqrt(I))
    return {
        "phi": bf(np.random.standard_normal((R, I)) * c / s[None, :]),
        "chi": bf(np.random.standard_normal((R, I)) * c * s[None, :]),
        "f": bf(np.random.uniform(0.2, 2.0, I)),
        "vker": bf(np.random.standard_normal((R, R)) / np.sqrt(R) * t[None, :]),
        "w": bf(np.random.uniform(0.5, 1.5, R) / t),
        "psi": bf(np.random.standard_normal((R, J))),
        "dv": bf(np.random.standard_normal(R)),
    }


def core(phi, chi, f, vker, w, psi, dv):
    psi = f64(psi)
    dp = first_order_density(f64(phi), f64(chi), f64(f))
    m = f64(vker) * dp
    g = f64(w)[:, None] * psi
    k = mxq(m, 1, "e4m3") @ mxq(g, 0, "e4m3")
    return f64(dv)[:, None] * psi - 0.5 * k


def reference(phi, chi, f, vker, w, psi, dv):
    R_out = core(phi, chi, f, vker, w, psi, dv)
    words, scales = planes(R_out)
    return R_out, words, scales

@@ -1,0 +1,236 @@
+from contextlib import ExitStack
+
+import concourse.mybir as mybir
+from concourse.masks import make_identity
+
+R, I, J = 1024, 512, 512
+FLOPS = 2 * R * R * I + 2 * R * R * J
+
+F32 = mybir.dt.float32
+BF16 = mybir.dt.bfloat16
+I32 = mybir.dt.int32
+U32 = mybir.dt.uint32
+U8 = mybir.dt.uint8
+FP8X4 = mybir.dt.float8_e4m3fn_x4
+MULT = mybir.AluOpType.mult
+ADD = mybir.AluOpType.add
+COPY = mybir.ActivationFunctionType.Copy
+
+P = 128
+BANKS = 8
+
+PAIRS = [("000", "010"), ("020", "030"), ("001", "011"), ("021", "031"),
+         ("100", "101"), ("110", "111"), ("120", "121"), ("130", "131")]
+
+ORDER = """TC00 TC01 CM00 CM01 TP00 TP01 QC01 PC00 QC00 TC10 PC01 QP00 QP01 TC11 D000 D010 CM10 TP10 CM11 PC10 QC10 TP11 PC11 M000 M010 QC11 DV00 TM0 MC0 DV01 D020 GM0 D030 QP10 QP11 DV03 D120 D001 D121 GI01 M020 M030 D101 GM1 D031 M001 QM0 M120 DV11 M101 D021 QG01 M031 D100 D111 D011 D110 M021 GI11 DV12 TM1 GI00 M121 GI10 TM3 M100 QG11 M011 M111 QG00 MC3 QG10 TM6 TM4 M110 TM2 D130 D131 TM5 MC1 QM3 QM1 MC2 QM2 M130 MC4 K02 QM4 DV02 MC6 K01 K03 DV13 M131 E02 K00 QM6 TM7 E01 MC5 QM5 DV10 K10 E03 E00 MC7 QM7 K11 K12 E11 OI01 K13 E12 E13 OI00 E10 QO01 OI11 OI10 QO00 QO11 QO10""".split()
+
+
+def tile_firstorderexchangeoperatorrealspaceactio_x1_kernel(
+    tc, phi, chi, f, vker, w, psi, dv, out_0, out_1, out_2
+):
+    nc = tc.nc
+    with ExitStack() as ctx:
+        sb = ctx.enter_context(tc.tile_pool(name="sb", bufs=1))
+        ps = ctx.enter_context(tc.psum_pool(name="ps", bufs=1))
+        ctx.enter_context(tc.manual_schedule())
+
+        chi_sb = sb.tile([P, 2, 4, I], BF16, align_bytes=64)
+        phi_sb = sb.tile([P, 2, 4, I], BF16, align_bytes=64)
+        psi_sb = sb.tile([P, 2, 4, J], BF16, align_bytes=64)
+        vker_sb = sb.tile([P, 2, 4, R], BF16, align_bytes=64)
+        f_sb = sb.tile([P, 4], BF16)
+        w_sb = sb.tile([P, 2, 16], BF16)
+        dv_sb = sb.tile([P, 2, 16], BF16)
+        dv_f32 = sb.tile([P, 2, 4], F32)
+        ident = sb.tile([P, P], F32, align_bytes=64)
+
+        c_t = sb.tile([P, R, 4], BF16, align_bytes=64)
+        phi_t = sb.tile([P, R, 4], BF16, align_bytes=64)
+        c_codes = sb.tile([P, R], U32, align_bytes=64)
+        c_scales = sb.tile([P, R], U8, align_bytes=64)
+        phi_codes = sb.tile([P, R], U32, align_bytes=64)
+        phi_scales = sb.tile([P, R], U8, align_bytes=64)
+        m_rows = sb.tile([P, 8, 2, 512], BF16, align_bytes=64)
+        m_t = sb.tile([P, 8, 256, 4], BF16, align_bytes=64)
+        m_codes = sb.tile([P, 8, 256], U32, align_bytes=64)
+        m_scales = sb.tile([P, 8, 256], U8, align_bytes=64)
+        g_rows = sb.tile([P, 2, 4, J], BF16, align_bytes=64)
+        g_t = sb.tile([P, 2, J, 4], BF16, align_bytes=64)
+        g_codes = sb.tile([P, 2, J], U32, align_bytes=64)
+        g_scales = sb.tile([P, 2, J], U8, align_bytes=64)
+        dv_psi = sb.tile([P, 2, 4, J], F32, align_bytes=64)
+        res = sb.tile([P, 2, 4, J], F32, align_bytes=64)
+        res_t = sb.tile([P, 2, J, 4], BF16, align_bytes=64)
+        res_codes = sb.tile([P, 2, J], U32, align_bytes=64)
+        res_scales = sb.tile([P, 2, J], U8, align_bytes=64)
+
+        def rows(x):
+            return x.rearrange("(g p t) c -> g p t c", g=2, t=4)
+
+        nc.scalar.dma_start(out=f_sb[:], in_=f.rearrange("(p t) -> p t", t=4))
+        nc.scalar.dma_start(out=dv_sb[:, :, 0:4], in_=dv.rearrange("(g p t) -> p g t", g=2, t=4))
+        nc.scalar.dma_start(out=w_sb[:, :, 0:4], in_=w.rearrange("(g p t) -> p g t", g=2, t=4))
+        make_identity(nc, ident[:])
+        nc.sync.dma_start(out=chi_sb[:, 0, 0:2, :], in_=rows(chi)[0][:, 0:2, :])
+        nc.sync.dma_start(out=chi_sb[:, 0, 2:4, :], in_=rows(chi)[0][:, 2:4, :])
+        nc.sync.dma_start(out=phi_sb[:, 0, 0:2, :], in_=rows(phi)[0][:, 0:2, :])
+        nc.sync.dma_start(out=phi_sb[:, 0, 2:4, :], in_=rows(phi)[0][:, 2:4, :])
+        nc.sync.dma_start(out=chi_sb[:, 1], in_=rows(chi)[1])
+        nc.sync.dma_start(out=vker_sb[:, 0, :, 0:512], in_=rows(vker)[0][:, :, 0:512])
+        nc.sync.dma_start(out=phi_sb[:, 1], in_=rows(phi)[1])
+        nc.sync.dma_start(out=psi_sb[:, 0], in_=rows(psi)[0])
+        nc.sync.dma_start(out=vker_sb[:, 0, :, 512:1024], in_=rows(vker)[0][:, :, 512:1024])
+        nc.sync.dma_start(out=psi_sb[:, 1], in_=rows(psi)[1])
+        nc.sync.dma_start(out=vker_sb[:, 1, :, 0:512], in_=rows(vker)[1][:, :, 0:512])
+        nc.sync.dma_start(out=vker_sb[:, 1, :, 512:1024], in_=rows(vker)[1][:, :, 512:1024])
+        nc.scalar.activation(out=dv_f32[:], in_=dv_sb[:, :, 0:4], func=COPY)
+
+        banks = {}
+
+        def new_bank(key):
+            tag = "bank%d" % (len(banks) % BANKS)
+            banks[key] = ps.tile([P, 512], F32, name=tag, tag=tag)
+            return banks[key]
+
+        place = {}
+        for n, pair in enumerate(PAIRS):
+            for s, key in enumerate(pair):
+                place[key] = (n, s)
+
+        def transpose_input(key, src, g, a):
+            bank = new_bank(key)
+            for s in range(2):
+                words = src[:, g, 2 * a + s, :].bitcast(F32)
+                for u in range(2):
+                    col = 256 * u + 128 * s
+                    nc.tensor.transpose(bank[:, col : col + 128], words[:, u:256:2], ident[:])
+
+        def words_out(dst, bank):
+            nc.scalar.copy(
+                out=dst.rearrange("p n j -> p (n j)").bitcast(F32).rearrange("p (n u) -> p n u", u=2),
+                in_=bank[:].rearrange("p (u n) -> p n u", u=2),
+            )
+
+        def quantize(codes, scales, src):
+            nc.vector.quantize_mx(
+                out=codes.bitcast(FP8X4), scales=scales, in_=src.rearrange("p n j -> p (n j)")
+            )
+
+        def interleave(copy, dst, src):
+            copy(
+                out=dst.rearrange("p (c i) t -> p c t i", i=4),
+                in_=src.rearrange("p t (c i) -> p c t i", i=4),
+            )
+
+        def mx(bank, lc, ls, rc, rs, first):
+            nc.tensor.matmul_mx(
+                out=bank[:], lhsT=lc.bitcast(FP8X4), lhsT_scale=ls, rhs=rc.bitcast(FP8X4),
+                rhs_scale=rs, start=first, stop=not first,
+            )
+
+        for step in ORDER:
+            kind = "".join(ch for ch in step if ch not in "0123456789")
+            key = step[len(kind) :]
+            idx = [int(ch) for ch in key]
+            if kind in ("TC", "TP", "CM", "PC", "QC", "QP"):
+                g, a = idx
+                cols = slice(512 * g + 256 * a, 512 * g + 256 * a + 256)
+                if kind == "TC":
+                    transpose_input("TC" + key, chi_sb, g, a)
+                elif kind == "TP":
+                    transpose_input("TP" + key, phi_sb, g, a)
+                elif kind == "CM":
+                    nc.vector.tensor_tensor(
+                        out=c_t[:, cols, :].rearrange("p n (u e) -> p n u e", u=2),
+                        in0=banks["TC" + key][:].bitcast(BF16).rearrange("p (u n e) -> p n u e", u=2, e=2),
+                        in1=f_sb[:].rearrange("p (o u e) -> p o u e", o=1, u=2).to_broadcast([P, 256, 2, 2]),
+                        op=MULT,
+                    )
+                elif kind == "PC":
+                    words_out(phi_t[:, cols, :], banks["TP" + key])
+                elif kind == "QC":
+                    quantize(c_codes[:, cols], c_scales[:, cols], c_t[:, cols, :])
+                else:
+                    quantize(phi_codes[:, cols], phi_scales[:, cols], phi_t[:, cols, :])
+            elif kind == "D":
+                g, t, h = idx
+                bank = new_bank(step)
+                r = slice(512 * g + 128 * t, 512 * g + 128 * t + 128)
+                q = slice(512 * h, 512 * h + 512)
+                mx(bank, phi_codes[:, r], phi_scales[:, r], c_codes[:, q], c_scales[:, q], True)
+                mx(bank, c_codes[:, r], c_scales[:, r], phi_codes[:, q], phi_scales[:, q], False)
+            elif kind == "M":
+                g, t, h = idx
+                n, s = place[key]
+                nc.vector.tensor_tensor(
+                    out=m_rows[:, n, s, :].rearrange("r (u p e) -> r u p e", u=2, e=2),
+                    in0=banks["D" + key][:].rearrange("r (u e p) -> r u p e", u=2, e=2),
+                    in1=vker_sb[:, g, t, 512 * h : 512 * h + 512].rearrange("r (p u e) -> r u p e", u=2, e=2),
+                    op=MULT,
+                )
+            elif kind == "TM":
+                n = idx[0]
+                bank = new_bank(step)
+                for s in range(2):
+                    words = m_rows[:, n, s, :].bitcast(F32)
+                    for u in range(2):
+                        col = 256 * u + 128 * s
+                        nc.tensor.transpose(bank[:, col : col + 128], words[:, 128 * u : 128 * u + 128], ident[:])
+            elif kind == "MC":
+                words_out(m_t[:, idx[0]], banks["TM" + key])
+            elif kind == "QM":
+                n = idx[0]
+                quantize(m_codes[:, n], m_scales[:, n], m_t[:, n])
+            elif kind == "GM":
+                h = idx[0]
+                for t in range(4):
+                    nc.vector.tensor_scalar(
+                        out=g_rows[:, h, t, :], in0=psi_sb[:, h, t, :], scalar1=w_sb[:, h, t : t + 1],
+                        scalar2=None, op0=MULT,
+                    )
+            elif kind == "GI":
+                h, a = idx
+                j = slice(256 * a, 256 * a + 256)
+                interleave(nc.scalar.copy, g_t[:, h, j, :], g_rows[:, h, :, j])
+            elif kind == "QG":
+                h, a = idx
+                j = slice(256 * a, 256 * a + 256)
+                quantize(g_codes[:, h, j], g_scales[:, h, j], g_t[:, h, j, :])
+            elif kind == "DV":
+                g, t = idx
+                nc.scalar.activation(
+                    out=dv_psi[:, g, t, :], in_=psi_sb[:, g, t, :], func=COPY, scale=dv_f32[:, g, t : t + 1]
+                )
+            elif kind == "K":
+                g, t = idx
+                bank = new_bank(step)
+                for h in range(2):
+                    n, s = place["%d%d%d" % (g, t, h)]
+                    r = slice(128 * s, 128 * s + 128)
+                    mx(bank, m_codes[:, n, r], m_scales[:, n, r], g_codes[:, h], g_scales[:, h], h == 0)
+            elif kind == "E":
+                g, t = idx
+                nc.vector.scalar_tensor_tensor(
+                    out=res[:, g, t, :], in0=banks["K" + key][:], scalar=-0.5, in1=dv_psi[:, g, t, :],
+                    op0=MULT, op1=ADD,
+                )
+                nc.sync.dma_start(out=rows(out_0)[g][:, t, :], in_=res[:, g, t, :])
+            elif kind == "OI":
+                g, a = idx
+                j = slice(256 * a, 256 * a + 256)
+                copy = nc.vector.tensor_copy if key == "11" else nc.scalar.copy
+                interleave(copy, res_t[:, g, j, :], res[:, g, :, j])
+            elif kind == "QO":
+                g, a = idx
+                j = slice(256 * a, 256 * a + 256)
+                quantize(res_codes[:, g, j], res_scales[:, g, j], res_t[:, g, j, :])
+                words = out_1[g].rearrange("p m t -> p (m t)").bitcast(I32)
+                nc.sync.dma_start(out=words[:, j], in_=res_codes[:, g, j].bitcast(I32))
+                other = "QO%d%d" % (g, 1 - a)
+                if ORDER.index(other) < ORDER.index(step):
+                    for quad in range(4):
+                        queue = nc.sync if quad % 2 == 0 or g == 0 else nc.scalar
+                        queue.dma_start(
+                            out=out_2[g, 4 * quad : 4 * quad + 4, :].bitcast(I32),
+                            in_=res_scales[32 * quad : 32 * quad + 4, g, :].bitcast(I32),
+                        )

@@ -19,10 +19,16 @@ COPY = mybir.ActivationFunctionType.Copy
 P = 128
 BANKS = 8
 
-PAIRS = [("000", "010"), ("020", "030"), ("001", "011"), ("021", "031"),
-         ("100", "101"), ("110", "111"), ("120", "121"), ("130", "131")]
+PAIRS = [("%d%d0" % (g, t), "%d%d1" % (g, t)) for g in range(2) for t in range(4)]
 
-ORDER = """TC00 TC01 CM00 CM01 TP00 TP01 QC01 PC00 QC00 TC10 PC01 QP00 QP01 TC11 D000 D010 CM10 TP10 CM11 PC10 QC10 TP11 PC11 M000 M010 QC11 DV00 TM0 MC0 DV01 D020 GM0 D030 QP10 QP11 DV03 D120 D001 D121 GI01 M020 M030 D101 GM1 D031 M001 QM0 M120 DV11 M101 D021 QG01 M031 D100 D111 D011 D110 M021 GI11 DV12 TM1 GI00 M121 GI10 TM3 M100 QG11 M011 M111 QG00 MC3 QG10 TM6 TM4 M110 TM2 D130 D131 TM5 MC1 QM3 QM1 MC2 QM2 M130 MC4 K02 QM4 DV02 MC6 K01 K03 DV13 M131 E02 K00 QM6 TM7 E01 MC5 QM5 DV10 K10 E03 E00 MC7 QM7 K11 K12 E11 OI01 K13 E12 E13 OI00 E10 QO01 OI11 OI10 QO00 QO11 QO10""".split()
+ORDER = """TC00 TC01 TP00 TP01 CM00 CM01 PC00 PC01 QC00 QC01 QP00 QP01
+TC10 TC11 CM10 CM11 TP10 TP11 PC10 PC11 DF QC10 QC11 D000 D010 D020 D030 QP10 M000 QP11 M010
+GM0 DV00 DV01 GI00 GI01 D001 D011 D021 D031 M020 M030 GM1 DV02 DV03 GI10 GI11
+D100 D101 D110 D111 M001 M011 M021 M031 D120 D121 TM0 TM1 QG00 M100 QG01 M101
+TM2 TM3 MC0 MC1 MC2 MC3 M110 M111 D130 D131 QG10 M120 QG11 M121
+DV10 TM4 TM5 TM6 MC4 MC5 MC6 DV11 QM0 QM1 M130 QM2 M131 QM3 QM4
+K00 K01 K02 TM7 K03 MC7 DV12 DV13 E00 QM5 E01 QM6 E02 E03 QM7
+K10 K11 K12 K13 OI00 OI01 E10 E11 E12 E13 QO00 OI10 OI11 QO01 QO11 QO10""".split()
 
 
 def tile_firstorderexchangeoperatorrealspaceactio_x1_kernel(
@@ -68,22 +74,21 @@ def tile_firstorderexchangeoperatorrealspaceactio_x1_kernel(
             return x.rearrange("(g p t) c -> g p t c", g=2, t=4)
 
         nc.scalar.dma_start(out=f_sb[:], in_=f.rearrange("(p t) -> p t", t=4))
-        nc.scalar.dma_start(out=dv_sb[:, :, 0:4], in_=dv.rearrange("(g p t) -> p g t", g=2, t=4))
-        nc.scalar.dma_start(out=w_sb[:, :, 0:4], in_=w.rearrange("(g p t) -> p g t", g=2, t=4))
         make_identity(nc, ident[:])
         nc.sync.dma_start(out=chi_sb[:, 0, 0:2, :], in_=rows(chi)[0][:, 0:2, :])
         nc.sync.dma_start(out=chi_sb[:, 0, 2:4, :], in_=rows(chi)[0][:, 2:4, :])
         nc.sync.dma_start(out=phi_sb[:, 0, 0:2, :], in_=rows(phi)[0][:, 0:2, :])
         nc.sync.dma_start(out=phi_sb[:, 0, 2:4, :], in_=rows(phi)[0][:, 2:4, :])
         nc.sync.dma_start(out=chi_sb[:, 1], in_=rows(chi)[1])
-        nc.sync.dma_start(out=vker_sb[:, 0, :, 0:512], in_=rows(vker)[0][:, :, 0:512])
         nc.sync.dma_start(out=phi_sb[:, 1], in_=rows(phi)[1])
+        nc.sync.dma_start(out=vker_sb[:, 0, 0:2, :], in_=rows(vker)[0][:, 0:2, :])
+        nc.sync.dma_start(out=dv_sb[:, :, 0:4], in_=dv.rearrange("(g p t) -> p g t", g=2, t=4))
+        nc.sync.dma_start(out=w_sb[:, :, 0:4], in_=w.rearrange("(g p t) -> p g t", g=2, t=4))
         nc.sync.dma_start(out=psi_sb[:, 0], in_=rows(psi)[0])
-        nc.sync.dma_start(out=vker_sb[:, 0, :, 512:1024], in_=rows(vker)[0][:, :, 512:1024])
+        nc.sync.dma_start(out=vker_sb[:, 0, 2:4, :], in_=rows(vker)[0][:, 2:4, :])
         nc.sync.dma_start(out=psi_sb[:, 1], in_=rows(psi)[1])
-        nc.sync.dma_start(out=vker_sb[:, 1, :, 0:512], in_=rows(vker)[1][:, :, 0:512])
-        nc.sync.dma_start(out=vker_sb[:, 1, :, 512:1024], in_=rows(vker)[1][:, :, 512:1024])
-        nc.scalar.activation(out=dv_f32[:], in_=dv_sb[:, :, 0:4], func=COPY)
+        nc.sync.dma_start(out=vker_sb[:, 1, 0:2, :], in_=rows(vker)[1][:, 0:2, :])
+        nc.sync.dma_start(out=vker_sb[:, 1, 2:4, :], in_=rows(vker)[1][:, 2:4, :])
 
         banks = {}
 
@@ -152,6 +157,8 @@ def tile_firstorderexchangeoperatorrealspaceactio_x1_kernel(
                     quantize(c_codes[:, cols], c_scales[:, cols], c_t[:, cols, :])
                 else:
                     quantize(phi_codes[:, cols], phi_scales[:, cols], phi_t[:, cols, :])
+            elif kind == "DF":
+                nc.scalar.activation(out=dv_f32[:], in_=dv_sb[:, :, 0:4], func=COPY)
             elif kind == "D":
                 g, t, h = idx
                 bank = new_bank(step)
@@ -225,12 +232,13 @@ def tile_firstorderexchangeoperatorrealspaceactio_x1_kernel(
                 j = slice(256 * a, 256 * a + 256)
                 quantize(res_codes[:, g, j], res_scales[:, g, j], res_t[:, g, j, :])
                 words = out_1[g].rearrange("p m t -> p (m t)").bitcast(I32)
-                nc.sync.dma_start(out=words[:, j], in_=res_codes[:, g, j].bitcast(I32))
-                other = "QO%d%d" % (g, 1 - a)
-                if ORDER.index(other) < ORDER.index(step):
-                    for quad in range(4):
-                        queue = nc.sync if quad % 2 == 0 or g == 0 else nc.scalar
-                        queue.dma_start(
-                            out=out_2[g, 4 * quad : 4 * quad + 4, :].bitcast(I32),
-                            in_=res_scales[32 * quad : 32 * quad + 4, g, :].bitcast(I32),
-                        )
+                if g == 1:
+                    nc.sync.dma_start(out=words[:, j], in_=res_codes[:, g, j].bitcast(I32))
+                elif a == 1:
+                    nc.sync.dma_start(out=words, in_=res_codes[:, g].bitcast(I32))
+        for quad in range(4):
+            queue = nc.scalar if quad < 2 else nc.sync
+            queue.dma_start(
+                out=out_2[:, 4 * quad : 4 * quad + 4, :].rearrange("g r m -> r g m").bitcast(I32),
+                in_=res_scales[32 * quad : 32 * quad + 4].bitcast(I32),
+            )

@@ -17,18 +17,14 @@ ADD = mybir.AluOpType.add
 COPY = mybir.ActivationFunctionType.Copy
 
 P = 128
+PACK = 4
+PASS = P * PACK
+GROUPS = R // PASS
+TILES = GROUPS * PACK
+HALF = PASS // 2
 BANKS = 8
-
-PAIRS = [("%d%d0" % (g, t), "%d%d1" % (g, t)) for g in range(2) for t in range(4)]
-
-ORDER = """TC00 TC01 TP00 TP01 CM00 CM01 PC00 PC01 QC00 QC01 QP00 QP01
-TC10 TC11 CM10 CM11 TP10 TP11 PC10 PC11 DF QC10 QC11 D000 D010 D020 D030 QP10 M000 QP11 M010
-GM0 DV00 DV01 GI00 GI01 D001 D011 D021 D031 M020 M030 GM1 DV02 DV03 GI10 GI11
-D100 D101 D110 D111 M001 M011 M021 M031 D120 D121 TM0 TM1 QG00 M100 QG01 M101
-TM2 TM3 MC0 MC1 MC2 MC3 M110 M111 D130 D131 QG10 M120 QG11 M121
-DV10 TM4 TM5 TM6 MC4 MC5 MC6 DV11 QM0 QM1 M130 QM2 M131 QM3 QM4
-K00 K01 K02 TM7 K03 MC7 DV12 DV13 E00 QM5 E01 QM6 E02 E03 QM7
-K10 K11 K12 K13 OI00 OI01 E10 E11 E12 E13 QO00 OI10 OI11 QO01 QO11 QO10""".split()
+QUADRANT = 32
+PADDED = 16
 
 
 def tile_firstorderexchangeoperatorrealspaceactio_x1_kernel(
@@ -40,75 +36,69 @@ def tile_firstorderexchangeoperatorrealspaceactio_x1_kernel(
         ps = ctx.enter_context(tc.psum_pool(name="ps", bufs=1))
         ctx.enter_context(tc.manual_schedule())
 
-        chi_sb = sb.tile([P, 2, 4, I], BF16, align_bytes=64)
-        phi_sb = sb.tile([P, 2, 4, I], BF16, align_bytes=64)
-        psi_sb = sb.tile([P, 2, 4, J], BF16, align_bytes=64)
-        vker_sb = sb.tile([P, 2, 4, R], BF16, align_bytes=64)
-        f_sb = sb.tile([P, 4], BF16)
-        w_sb = sb.tile([P, 2, 16], BF16)
-        dv_sb = sb.tile([P, 2, 16], BF16)
-        dv_f32 = sb.tile([P, 2, 4], F32)
+        chi_sb = sb.tile([P, GROUPS, PACK, I], BF16, align_bytes=64)
+        phi_sb = sb.tile([P, GROUPS, PACK, I], BF16, align_bytes=64)
+        psi_sb = sb.tile([P, GROUPS, PACK, J], BF16, align_bytes=64)
+        vker_sb = sb.tile([P, GROUPS, PACK, R], BF16, align_bytes=64)
+        f_sb = sb.tile([P, PACK], BF16)
+        w_sb = sb.tile([P, GROUPS, PADDED], BF16)
+        dv_sb = sb.tile([P, GROUPS, PADDED], BF16)
+        dv_f32 = sb.tile([P, GROUPS, PACK], F32)
         ident = sb.tile([P, P], F32, align_bytes=64)
 
-        c_t = sb.tile([P, R, 4], BF16, align_bytes=64)
-        phi_t = sb.tile([P, R, 4], BF16, align_bytes=64)
+        c_t = sb.tile([P, R, PACK], BF16, align_bytes=64)
+        phi_t = sb.tile([P, R, PACK], BF16, align_bytes=64)
         c_codes = sb.tile([P, R], U32, align_bytes=64)
         c_scales = sb.tile([P, R], U8, align_bytes=64)
         phi_codes = sb.tile([P, R], U32, align_bytes=64)
         phi_scales = sb.tile([P, R], U8, align_bytes=64)
-        m_rows = sb.tile([P, 8, 2, 512], BF16, align_bytes=64)
-        m_t = sb.tile([P, 8, 256, 4], BF16, align_bytes=64)
-        m_codes = sb.tile([P, 8, 256], U32, align_bytes=64)
-        m_scales = sb.tile([P, 8, 256], U8, align_bytes=64)
-        g_rows = sb.tile([P, 2, 4, J], BF16, align_bytes=64)
-        g_t = sb.tile([P, 2, J, 4], BF16, align_bytes=64)
-        g_codes = sb.tile([P, 2, J], U32, align_bytes=64)
-        g_scales = sb.tile([P, 2, J], U8, align_bytes=64)
-        dv_psi = sb.tile([P, 2, 4, J], F32, align_bytes=64)
-        res = sb.tile([P, 2, 4, J], F32, align_bytes=64)
-        res_t = sb.tile([P, 2, J, 4], BF16, align_bytes=64)
-        res_codes = sb.tile([P, 2, J], U32, align_bytes=64)
-        res_scales = sb.tile([P, 2, J], U8, align_bytes=64)
+        m_rows = sb.tile([P, TILES, GROUPS, PASS], BF16, align_bytes=64)
+        m_t = sb.tile([P, TILES, HALF, PACK], BF16, align_bytes=64)
+        m_codes = sb.tile([P, TILES, HALF], U32, align_bytes=64)
+        m_scales = sb.tile([P, TILES, HALF], U8, align_bytes=64)
+        g_rows = sb.tile([P, GROUPS, PACK, J], BF16, align_bytes=64)
+        g_t = sb.tile([P, GROUPS, J, PACK], BF16, align_bytes=64)
+        g_codes = sb.tile([P, GROUPS, J], U32, align_bytes=64)
+        g_scales = sb.tile([P, GROUPS, J], U8, align_bytes=64)
+        dv_psi = sb.tile([P, GROUPS, PACK, J], F32, align_bytes=64)
+        res = sb.tile([P, GROUPS, PACK, J], F32, align_bytes=64)
+        res_t = sb.tile([P, GROUPS, J, PACK], BF16, align_bytes=64)
+        res_codes = sb.tile([P, GROUPS, J], U32, align_bytes=64)
+        res_scales = sb.tile([P, GROUPS, J], U8, align_bytes=64)
 
         def rows(x):
-            return x.rearrange("(g p t) c -> g p t c", g=2, t=4)
+            return x.rearrange("(g p t) c -> g p t c", g=GROUPS, t=PACK)
 
-        nc.scalar.dma_start(out=f_sb[:], in_=f.rearrange("(p t) -> p t", t=4))
-        make_identity(nc, ident[:])
-        nc.sync.dma_start(out=chi_sb[:, 0, 0:2, :], in_=rows(chi)[0][:, 0:2, :])
-        nc.sync.dma_start(out=chi_sb[:, 0, 2:4, :], in_=rows(chi)[0][:, 2:4, :])
-        nc.sync.dma_start(out=phi_sb[:, 0, 0:2, :], in_=rows(phi)[0][:, 0:2, :])
-        nc.sync.dma_start(out=phi_sb[:, 0, 2:4, :], in_=rows(phi)[0][:, 2:4, :])
-        nc.sync.dma_start(out=chi_sb[:, 1], in_=rows(chi)[1])
-        nc.sync.dma_start(out=phi_sb[:, 1], in_=rows(phi)[1])
-        nc.sync.dma_start(out=vker_sb[:, 0, 0:2, :], in_=rows(vker)[0][:, 0:2, :])
-        nc.sync.dma_start(out=dv_sb[:, :, 0:4], in_=dv.rearrange("(g p t) -> p g t", g=2, t=4))
-        nc.sync.dma_start(out=w_sb[:, :, 0:4], in_=w.rearrange("(g p t) -> p g t", g=2, t=4))
-        nc.sync.dma_start(out=psi_sb[:, 0], in_=rows(psi)[0])
-        nc.sync.dma_start(out=vker_sb[:, 0, 2:4, :], in_=rows(vker)[0][:, 2:4, :])
-        nc.sync.dma_start(out=psi_sb[:, 1], in_=rows(psi)[1])
-        nc.sync.dma_start(out=vker_sb[:, 1, 0:2, :], in_=rows(vker)[1][:, 0:2, :])
-        nc.sync.dma_start(out=vker_sb[:, 1, 2:4, :], in_=rows(vker)[1][:, 2:4, :])
+        def load_pair(dst, src, g, a):
+            slots = slice(2 * a, 2 * a + 2)
+            nc.sync.dma_start(out=dst[:, g, slots, :], in_=rows(src)[g][:, slots, :])
+
+        def load_group(dst, src, g):
+            nc.sync.dma_start(out=dst[:, g], in_=rows(src)[g])
+
+        def load_vector(dst, src):
+            nc.sync.dma_start(out=dst[:, :, 0:PACK], in_=src.rearrange("(g p t) -> p g t", g=GROUPS, t=PACK))
 
         banks = {}
 
         def new_bank(key):
             tag = "bank%d" % (len(banks) % BANKS)
-            banks[key] = ps.tile([P, 512], F32, name=tag, tag=tag)
+            banks[key] = ps.tile([P, PASS], F32, name=tag, tag=tag)
             return banks[key]
 
-        place = {}
-        for n, pair in enumerate(PAIRS):
-            for s, key in enumerate(pair):
-                place[key] = (n, s)
+        def pair_cols(g, a):
+            return slice(PASS * g + HALF * a, PASS * g + HALF * (a + 1))
 
-        def transpose_input(key, src, g, a):
-            bank = new_bank(key)
+        def half(a):
+            return slice(HALF * a, HALF * (a + 1))
+
+        def turn_input(name, src, g, a):
+            bank = new_bank((name, g, a))
             for s in range(2):
                 words = src[:, g, 2 * a + s, :].bitcast(F32)
                 for u in range(2):
-                    col = 256 * u + 128 * s
-                    nc.tensor.transpose(bank[:, col : col + 128], words[:, u:256:2], ident[:])
+                    col = HALF * u + P * s
+                    nc.tensor.transpose(bank[:, col : col + P], words[:, u : I // 2 : 2], ident[:])
 
         def words_out(dst, bank):
             nc.scalar.copy(
@@ -127,118 +117,214 @@ def tile_firstorderexchangeoperatorrealspaceactio_x1_kernel(
                 in_=src.rearrange("p t (c i) -> p c t i", i=4),
             )
 
-        def mx(bank, lc, ls, rc, rs, first):
+        def mx_pass(bank, lhs_codes, lhs_scales, rhs_codes, rhs_scales, first):
             nc.tensor.matmul_mx(
-                out=bank[:], lhsT=lc.bitcast(FP8X4), lhsT_scale=ls, rhs=rc.bitcast(FP8X4),
-                rhs_scale=rs, start=first, stop=not first,
+                out=bank[:], lhsT=lhs_codes.bitcast(FP8X4), lhsT_scale=lhs_scales,
+                rhs=rhs_codes.bitcast(FP8X4), rhs_scale=rhs_scales, start=first, stop=not first,
             )
 
-        for step in ORDER:
-            kind = "".join(ch for ch in step if ch not in "0123456789")
-            key = step[len(kind) :]
-            idx = [int(ch) for ch in key]
-            if kind in ("TC", "TP", "CM", "PC", "QC", "QP"):
-                g, a = idx
-                cols = slice(512 * g + 256 * a, 512 * g + 256 * a + 256)
-                if kind == "TC":
-                    transpose_input("TC" + key, chi_sb, g, a)
-                elif kind == "TP":
-                    transpose_input("TP" + key, phi_sb, g, a)
-                elif kind == "CM":
-                    nc.vector.tensor_tensor(
-                        out=c_t[:, cols, :].rearrange("p n (u e) -> p n u e", u=2),
-                        in0=banks["TC" + key][:].bitcast(BF16).rearrange("p (u n e) -> p n u e", u=2, e=2),
-                        in1=f_sb[:].rearrange("p (o u e) -> p o u e", o=1, u=2).to_broadcast([P, 256, 2, 2]),
-                        op=MULT,
-                    )
-                elif kind == "PC":
-                    words_out(phi_t[:, cols, :], banks["TP" + key])
-                elif kind == "QC":
-                    quantize(c_codes[:, cols], c_scales[:, cols], c_t[:, cols, :])
-                else:
-                    quantize(phi_codes[:, cols], phi_scales[:, cols], phi_t[:, cols, :])
-            elif kind == "DF":
-                nc.scalar.activation(out=dv_f32[:], in_=dv_sb[:, :, 0:4], func=COPY)
-            elif kind == "D":
-                g, t, h = idx
-                bank = new_bank(step)
-                r = slice(512 * g + 128 * t, 512 * g + 128 * t + 128)
-                q = slice(512 * h, 512 * h + 512)
-                mx(bank, phi_codes[:, r], phi_scales[:, r], c_codes[:, q], c_scales[:, q], True)
-                mx(bank, c_codes[:, r], c_scales[:, r], phi_codes[:, q], phi_scales[:, q], False)
-            elif kind == "M":
-                g, t, h = idx
-                n, s = place[key]
-                nc.vector.tensor_tensor(
-                    out=m_rows[:, n, s, :].rearrange("r (u p e) -> r u p e", u=2, e=2),
-                    in0=banks["D" + key][:].rearrange("r (u e p) -> r u p e", u=2, e=2),
-                    in1=vker_sb[:, g, t, 512 * h : 512 * h + 512].rearrange("r (p u e) -> r u p e", u=2, e=2),
-                    op=MULT,
-                )
-            elif kind == "TM":
-                n = idx[0]
-                bank = new_bank(step)
-                for s in range(2):
-                    words = m_rows[:, n, s, :].bitcast(F32)
-                    for u in range(2):
-                        col = 256 * u + 128 * s
-                        nc.tensor.transpose(bank[:, col : col + 128], words[:, 128 * u : 128 * u + 128], ident[:])
-            elif kind == "MC":
-                words_out(m_t[:, idx[0]], banks["TM" + key])
-            elif kind == "QM":
-                n = idx[0]
-                quantize(m_codes[:, n], m_scales[:, n], m_t[:, n])
-            elif kind == "GM":
-                h = idx[0]
-                for t in range(4):
+        def make_c(g, a):
+            nc.vector.tensor_tensor(
+                out=c_t[:, pair_cols(g, a), :].rearrange("p n (u e) -> p n u e", u=2),
+                in0=banks["chi", g, a][:].bitcast(BF16).rearrange("p (u n e) -> p n u e", u=2, e=2),
+                in1=f_sb[:].rearrange("p (o u e) -> p o u e", o=1, u=2).to_broadcast([P, HALF, 2, 2]),
+                op=MULT,
+            )
+
+        def quantize_c(g, a):
+            cols = pair_cols(g, a)
+            quantize(c_codes[:, cols], c_scales[:, cols], c_t[:, cols, :])
+
+        def quantize_phi(g, a):
+            cols = pair_cols(g, a)
+            quantize(phi_codes[:, cols], phi_scales[:, cols], phi_t[:, cols, :])
+
+        def dp_tile(g, t, h):
+            bank = new_bank(("dp", g, t, h))
+            r = slice(PASS * g + P * t, PASS * g + P * (t + 1))
+            q = slice(PASS * h, PASS * (h + 1))
+            mx_pass(bank, phi_codes[:, r], phi_scales[:, r], c_codes[:, q], c_scales[:, q], True)
+            mx_pass(bank, c_codes[:, r], c_scales[:, r], phi_codes[:, q], phi_scales[:, q], False)
+
+        def make_m(g, t, h):
+            nc.vector.tensor_tensor(
+                out=m_rows[:, PACK * g + t, h, :].rearrange("r (u p e) -> r u p e", u=2, e=2),
+                in0=banks["dp", g, t, h][:].rearrange("r (u e p) -> r u p e", u=2, e=2),
+                in1=vker_sb[:, g, t, PASS * h : PASS * (h + 1)].rearrange("r (p u e) -> r u p e", u=2, e=2),
+                op=MULT,
+            )
+
+        def turn_m(n):
+            bank = new_bank(("m", n))
+            for h in range(GROUPS):
+                words = m_rows[:, n, h, :].bitcast(F32)
+                for u in range(2):
+                    col = HALF * u + P * h
+                    nc.tensor.transpose(bank[:, col : col + P], words[:, P * u : P * (u + 1)], ident[:])
+
+        def copy_m(n):
+            words_out(m_t[:, n], banks["m", n])
+
+        def quantize_m(n, count):
+            tiles = slice(n, n + count)
+            quantize(
+                m_codes[:, tiles].rearrange("p n c -> p (n c)"),
+                m_scales[:, tiles].rearrange("p n c -> p (n c)"),
+                m_t[:, tiles].rearrange("p n c j -> p (n c) j"),
+            )
+
+        def interleave_g(h):
+            for a in range(2):
+                interleave(nc.scalar.copy, g_t[:, h, half(a), :], g_rows[:, h, :, half(a)])
+
+        def quantize_g(h):
+            quantize(g_codes[:, h], g_scales[:, h], g_t[:, h])
+
+        def make_dv_psi(g, t):
+            nc.scalar.activation(
+                out=dv_psi[:, g, t, :], in_=psi_sb[:, g, t, :], func=COPY, scale=dv_f32[:, g, t : t + 1]
+            )
+
+        def k_tile(g, t):
+            bank = new_bank(("k", g, t))
+            n = PACK * g + t
+            for h in range(GROUPS):
+                r = slice(P * h, P * (h + 1))
+                mx_pass(bank, m_codes[:, n, r], m_scales[:, n, r], g_codes[:, h], g_scales[:, h], h == 0)
+
+        def finish(g, t):
+            nc.vector.scalar_tensor_tensor(
+                out=res[:, g, t, :], in0=banks["k", g, t][:], scalar=-0.5, in1=dv_psi[:, g, t, :],
+                op0=MULT, op1=ADD,
+            )
+            nc.sync.dma_start(out=rows(out_0)[g][:, t, :], in_=res[:, g, t, :])
+
+        def interleave_res(copy, g, a):
+            interleave(copy, res_t[:, g, half(a), :], res[:, g, :, half(a)])
+
+        def quantize_res(g, a):
+            quantize(res_codes[:, g, half(a)], res_scales[:, g, half(a)], res_t[:, g, half(a), :])
+
+        def store_codes(g, cols):
+            words = out_1[g].rearrange("p m t -> p (m t)").bitcast(I32)
+            nc.sync.dma_start(out=words[:, cols], in_=res_codes[:, g, cols].bitcast(I32))
+
+        nc.scalar.dma_start(out=f_sb[:], in_=f.rearrange("(p t) -> p t", t=PACK))
+        make_identity(nc, ident[:])
+        for dst, src in ((chi_sb, chi), (phi_sb, phi)):
+            for a in range(2):
+                load_pair(dst, src, 0, a)
+        load_group(chi_sb, chi, 1)
+        load_group(phi_sb, phi, 1)
+        load_vector(w_sb, w)
+        load_group(psi_sb, psi, 0)
+        for a in range(2):
+            load_pair(vker_sb, vker, 0, a)
+        load_vector(dv_sb, dv)
+        load_group(psi_sb, psi, 1)
+        for a in range(2):
+            load_pair(vker_sb, vker, 1, a)
+
+        for g in range(GROUPS):
+            for name, src in (("chi", chi_sb), ("phi", phi_sb)):
+                for a in range(2):
+                    turn_input(name, src, g, a)
+            for a in range(2):
+                make_c(g, a)
+            for a in range(2):
+                words_out(phi_t[:, pair_cols(g, a), :], banks["phi", g, a])
+            for a in range(2):
+                quantize_c(g, a)
+            if g == GROUPS - 1:
+                for t in range(PACK):
                     nc.vector.tensor_scalar(
-                        out=g_rows[:, h, t, :], in0=psi_sb[:, h, t, :], scalar1=w_sb[:, h, t : t + 1],
+                        out=g_rows[:, 0, t, :], in0=psi_sb[:, 0, t, :], scalar1=w_sb[:, 0, t : t + 1],
                         scalar2=None, op0=MULT,
                     )
-            elif kind == "GI":
-                h, a = idx
-                j = slice(256 * a, 256 * a + 256)
-                interleave(nc.scalar.copy, g_t[:, h, j, :], g_rows[:, h, :, j])
-            elif kind == "QG":
-                h, a = idx
-                j = slice(256 * a, 256 * a + 256)
-                quantize(g_codes[:, h, j], g_scales[:, h, j], g_t[:, h, j, :])
-            elif kind == "DV":
-                g, t = idx
-                nc.scalar.activation(
-                    out=dv_psi[:, g, t, :], in_=psi_sb[:, g, t, :], func=COPY, scale=dv_f32[:, g, t : t + 1]
-                )
-            elif kind == "K":
-                g, t = idx
-                bank = new_bank(step)
-                for h in range(2):
-                    n, s = place["%d%d%d" % (g, t, h)]
-                    r = slice(128 * s, 128 * s + 128)
-                    mx(bank, m_codes[:, n, r], m_scales[:, n, r], g_codes[:, h], g_scales[:, h], h == 0)
-            elif kind == "E":
-                g, t = idx
-                nc.vector.scalar_tensor_tensor(
-                    out=res[:, g, t, :], in0=banks["K" + key][:], scalar=-0.5, in1=dv_psi[:, g, t, :],
-                    op0=MULT, op1=ADD,
-                )
-                nc.sync.dma_start(out=rows(out_0)[g][:, t, :], in_=res[:, g, t, :])
-            elif kind == "OI":
-                g, a = idx
-                j = slice(256 * a, 256 * a + 256)
-                copy = nc.vector.tensor_copy if key == "11" else nc.scalar.copy
-                interleave(copy, res_t[:, g, j, :], res[:, g, :, j])
-            elif kind == "QO":
-                g, a = idx
-                j = slice(256 * a, 256 * a + 256)
-                quantize(res_codes[:, g, j], res_scales[:, g, j], res_t[:, g, j, :])
-                words = out_1[g].rearrange("p m t -> p (m t)").bitcast(I32)
-                if g == 1:
-                    nc.sync.dma_start(out=words[:, j], in_=res_codes[:, g, j].bitcast(I32))
-                elif a == 1:
-                    nc.sync.dma_start(out=words, in_=res_codes[:, g].bitcast(I32))
-        for quad in range(4):
+            for a in range(2):
+                quantize_phi(g, a)
+
+        for t in range(PACK):
+            nc.gpsimd.tensor_scalar(
+                out=g_rows[:, 1, t, :], in0=psi_sb[:, 1, t, :], scalar1=w_sb[:, 1, t : t + 1],
+                scalar2=0.0, op0=MULT, op1=ADD,
+            )
+        interleave_g(0)
+        nc.scalar.activation(out=dv_f32[:], in_=dv_sb[:, :, 0:PACK], func=COPY)
+        for t in range(PACK):
+            make_dv_psi(0, t)
+        make_dv_psi(1, 0)
+        interleave_g(1)
+
+        first = [(0, t, h) for h in range(GROUPS) for t in range(PACK)]
+        for tile in first:
+            dp_tile(*tile)
+        for t in range(PACK - 1):
+            make_m(*first[2 * t])
+            make_m(*first[2 * t + 1])
+            dp_tile(1, t, 0)
+            dp_tile(1, t, 1)
+        make_m(*first[-2])
+        make_m(*first[-1])
+        turn_m(0)
+        turn_m(1)
+        make_m(1, 0, 0)
+        make_m(1, 0, 1)
+        turn_m(2)
+        turn_m(3)
+        for n in range(PACK):
+            copy_m(n)
+        quantize_g(0)
+        make_m(1, 1, 0)
+        make_m(1, 1, 1)
+        dp_tile(1, 3, 0)
+        dp_tile(1, 3, 1)
+        quantize_g(1)
+        make_m(1, 2, 0)
+        make_m(1, 2, 1)
+        make_dv_psi(1, 1)
+        for n in range(PACK, TILES - 1):
+            turn_m(n)
+        for n in range(PACK, TILES - 1):
+            copy_m(n)
+        make_dv_psi(1, 2)
+        quantize_m(0, 2)
+        make_m(1, 3, 0)
+        quantize_m(2, 2)
+        make_m(1, 3, 1)
+        quantize_m(4, 1)
+
+        for t in range(PACK - 1):
+            k_tile(0, t)
+        turn_m(TILES - 1)
+        k_tile(0, PACK - 1)
+        copy_m(TILES - 1)
+        make_dv_psi(1, 3)
+        finish(0, 0)
+        quantize_m(5, 1)
+        finish(0, 1)
+        quantize_m(6, 1)
+        finish(0, 2)
+        finish(0, 3)
+        quantize_m(7, 1)
+        for t in range(PACK):
+            k_tile(1, t)
+        for a in range(2):
+            interleave_res(nc.scalar.copy, 0, a)
+        for t in range(PACK):
+            finish(1, t)
+
+        quantize_res(0, 0)
+        interleave_res(nc.scalar.copy, 1, 0)
+        interleave_res(nc.vector.tensor_copy, 1, 1)
+        quantize_res(0, 1)
+        store_codes(0, slice(0, J))
+        for a in (1, 0):
+            quantize_res(1, a)
+            store_codes(1, half(a))
+        for quad in range(P // QUADRANT):
             queue = nc.scalar if quad < 2 else nc.sync
             queue.dma_start(
                 out=out_2[:, 4 * quad : 4 * quad + 4, :].rearrange("g r m -> r g m").bitcast(I32),
-                in_=res_scales[32 * quad : 32 * quad + 4].bitcast(I32),
+                in_=res_scales[QUADRANT * quad : QUADRANT * quad + 4].bitcast(I32),
             )

from contextlib import ExitStack

import concourse.mybir as mybir
from concourse.masks import make_identity

R, I, J = 1024, 512, 512
FLOPS = 2 * R * R * I + 2 * R * R * J

F32 = mybir.dt.float32
BF16 = mybir.dt.bfloat16
I32 = mybir.dt.int32
U32 = mybir.dt.uint32
U8 = mybir.dt.uint8
FP8X4 = mybir.dt.float8_e4m3fn_x4
MULT = mybir.AluOpType.mult
ADD = mybir.AluOpType.add
COPY = mybir.ActivationFunctionType.Copy

P = 128
PACK = 4
PASS = P * PACK
GROUPS = R // PASS
TILES = GROUPS * PACK
HALF = PASS // 2
BANKS = 8
QUADRANT = 32
PADDED = 16


def tile_firstorderexchangeoperatorrealspaceactio_x1_kernel(
    tc, phi, chi, f, vker, w, psi, dv, out_0, out_1, out_2
):
    nc = tc.nc
    with ExitStack() as ctx:
        sb = ctx.enter_context(tc.tile_pool(name="sb", bufs=1))
        ps = ctx.enter_context(tc.psum_pool(name="ps", bufs=1))
        ctx.enter_context(tc.manual_schedule())

        chi_sb = sb.tile([P, GROUPS, PACK, I], BF16, align_bytes=64)
        phi_sb = sb.tile([P, GROUPS, PACK, I], BF16, align_bytes=64)
        psi_sb = sb.tile([P, GROUPS, PACK, J], BF16, align_bytes=64)
        vker_sb = sb.tile([P, GROUPS, PACK, R], BF16, align_bytes=64)
        f_sb = sb.tile([P, PACK], BF16)
        w_sb = sb.tile([P, GROUPS, PADDED], BF16)
        dv_sb = sb.tile([P, GROUPS, PADDED], BF16)
        dv_f32 = sb.tile([P, GROUPS, PACK], F32)
        ident = sb.tile([P, P], F32, align_bytes=64)

        c_t = sb.tile([P, R, PACK], BF16, align_bytes=64)
        phi_t = sb.tile([P, R, PACK], BF16, align_bytes=64)
        c_codes = sb.tile([P, R], U32, align_bytes=64)
        c_scales = sb.tile([P, R], U8, align_bytes=64)
        phi_codes = sb.tile([P, R], U32, align_bytes=64)
        phi_scales = sb.tile([P, R], U8, align_bytes=64)
        m_rows = sb.tile([P, TILES, GROUPS, PASS], BF16, align_bytes=64)
        m_t = sb.tile([P, TILES, HALF, PACK], BF16, align_bytes=64)
        m_codes = sb.tile([P, TILES, HALF], U32, align_bytes=64)
        m_scales = sb.tile([P, TILES, HALF], U8, align_bytes=64)
        g_rows = sb.tile([P, GROUPS, PACK, J], BF16, align_bytes=64)
        g_t = sb.tile([P, GROUPS, J, PACK], BF16, align_bytes=64)
        g_codes = sb.tile([P, GROUPS, J], U32, align_bytes=64)
        g_scales = sb.tile([P, GROUPS, J], U8, align_bytes=64)
        dv_psi = sb.tile([P, GROUPS, PACK, J], F32, align_bytes=64)
        res = sb.tile([P, GROUPS, PACK, J], F32, align_bytes=64)
        res_t = sb.tile([P, GROUPS, J, PACK], BF16, align_bytes=64)
        res_codes = sb.tile([P, GROUPS, J], U32, align_bytes=64)
        res_scales = sb.tile([P, GROUPS, J], U8, align_bytes=64)

        def rows(x):
            return x.rearrange("(g p t) c -> g p t c", g=GROUPS, t=PACK)

        def load_pair(dst, src, g, a):
            slots = slice(2 * a, 2 * a + 2)
            nc.sync.dma_start(out=dst[:, g, slots, :], in_=rows(src)[g][:, slots, :])

        def load_group(dst, src, g):
            nc.sync.dma_start(out=dst[:, g], in_=rows(src)[g])

        def load_vector(dst, src):
            nc.sync.dma_start(out=dst[:, :, 0:PACK], in_=src.rearrange("(g p t) -> p g t", g=GROUPS, t=PACK))

        banks = {}

        def new_bank(key):
            tag = "bank%d" % (len(banks) % BANKS)
            banks[key] = ps.tile([P, PASS], F32, name=tag, tag=tag)
            return banks[key]

        def pair_cols(g, a):
            return slice(PASS * g + HALF * a, PASS * g + HALF * (a + 1))

        def half(a):
            return slice(HALF * a, HALF * (a + 1))

        def turn_input(name, src, g, a):
            bank = new_bank((name, g, a))
            for s in range(2):
                words = src[:, g, 2 * a + s, :].bitcast(F32)
                for u in range(2):
                    col = HALF * u + P * s
                    nc.tensor.transpose(bank[:, col : col + P], words[:, u : I // 2 : 2], ident[:])

        def words_out(dst, bank):
            nc.scalar.copy(
                out=dst.rearrange("p n j -> p (n j)").bitcast(F32).rearrange("p (n u) -> p n u", u=2),
                in_=bank[:].rearrange("p (u n) -> p n u", u=2),
            )

        def quantize(codes, scales, src):
            nc.vector.quantize_mx(
                out=codes.bitcast(FP8X4), scales=scales, in_=src.rearrange("p n j -> p (n j)")
            )

        def interleave(copy, dst, src):
            copy(
                out=dst.rearrange("p (c i) t -> p c t i", i=4),
                in_=src.rearrange("p t (c i) -> p c t i", i=4),
            )

        def mx_pass(bank, lhs_codes, lhs_scales, rhs_codes, rhs_scales, first):
            nc.tensor.matmul_mx(
                out=bank[:], lhsT=lhs_codes.bitcast(FP8X4), lhsT_scale=lhs_scales,
                rhs=rhs_codes.bitcast(FP8X4), rhs_scale=rhs_scales, start=first, stop=not first,
            )

        def make_c(g, a):
            nc.vector.tensor_tensor(
                out=c_t[:, pair_cols(g, a), :].rearrange("p n (u e) -> p n u e", u=2),
                in0=banks["chi", g, a][:].bitcast(BF16).rearrange("p (u n e) -> p n u e", u=2, e=2),
                in1=f_sb[:].rearrange("p (o u e) -> p o u e", o=1, u=2).to_broadcast([P, HALF, 2, 2]),
                op=MULT,
            )

        def quantize_c(g, a):
            cols = pair_cols(g, a)
            quantize(c_codes[:, cols], c_scales[:, cols], c_t[:, cols, :])

        def quantize_phi(g, a):
            cols = pair_cols(g, a)
            quantize(phi_codes[:, cols], phi_scales[:, cols], phi_t[:, cols, :])

        def dp_tile(g, t, h):
            bank = new_bank(("dp", g, t, h))
            r = slice(PASS * g + P * t, PASS * g + P * (t + 1))
            q = slice(PASS * h, PASS * (h + 1))
            mx_pass(bank, phi_codes[:, r], phi_scales[:, r], c_codes[:, q], c_scales[:, q], True)
            mx_pass(bank, c_codes[:, r], c_scales[:, r], phi_codes[:, q], phi_scales[:, q], False)

        def make_m(g, t, h):
            nc.vector.tensor_tensor(
                out=m_rows[:, PACK * g + t, h, :].rearrange("r (u p e) -> r u p e", u=2, e=2),
                in0=banks["dp", g, t, h][:].rearrange("r (u e p) -> r u p e", u=2, e=2),
                in1=vker_sb[:, g, t, PASS * h : PASS * (h + 1)].rearrange("r (p u e) -> r u p e", u=2, e=2),
                op=MULT,
            )

        def turn_m(n):
            bank = new_bank(("m", n))
            for h in range(GROUPS):
                words = m_rows[:, n, h, :].bitcast(F32)
                for u in range(2):
                    col = HALF * u + P * h
                    nc.tensor.transpose(bank[:, col : col + P], words[:, P * u : P * (u + 1)], ident[:])

        def copy_m(n):
            words_out(m_t[:, n], banks["m", n])

        def quantize_m(n, count):
            tiles = slice(n, n + count)
            quantize(
                m_codes[:, tiles].rearrange("p n c -> p (n c)"),
                m_scales[:, tiles].rearrange("p n c -> p (n c)"),
                m_t[:, tiles].rearrange("p n c j -> p (n c) j"),
            )

        def interleave_g(h):
            for a in range(2):
                interleave(nc.scalar.copy, g_t[:, h, half(a), :], g_rows[:, h, :, half(a)])

        def quantize_g(h):
            quantize(g_codes[:, h], g_scales[:, h], g_t[:, h])

        def make_dv_psi(g, t):
            nc.scalar.activation(
                out=dv_psi[:, g, t, :], in_=psi_sb[:, g, t, :], func=COPY, scale=dv_f32[:, g, t : t + 1]
            )

        def k_tile(g, t):
            bank = new_bank(("k", g, t))
            n = PACK * g + t
            for h in range(GROUPS):
                r = slice(P * h, P * (h + 1))
                mx_pass(bank, m_codes[:, n, r], m_scales[:, n, r], g_codes[:, h], g_scales[:, h], h == 0)

        def finish(g, t):
            nc.vector.scalar_tensor_tensor(
                out=res[:, g, t, :], in0=banks["k", g, t][:], scalar=-0.5, in1=dv_psi[:, g, t, :],
                op0=MULT, op1=ADD,
            )
            nc.sync.dma_start(out=rows(out_0)[g][:, t, :], in_=res[:, g, t, :])

        def interleave_res(copy, g, a):
            interleave(copy, res_t[:, g, half(a), :], res[:, g, :, half(a)])

        def quantize_res(g, a):
            quantize(res_codes[:, g, half(a)], res_scales[:, g, half(a)], res_t[:, g, half(a), :])

        def store_codes(g, cols):
            words = out_1[g].rearrange("p m t -> p (m t)").bitcast(I32)
            nc.sync.dma_start(out=words[:, cols], in_=res_codes[:, g, cols].bitcast(I32))

        nc.scalar.dma_start(out=f_sb[:], in_=f.rearrange("(p t) -> p t", t=PACK))
        make_identity(nc, ident[:])
        for dst, src in ((chi_sb, chi), (phi_sb, phi)):
            for a in range(2):
                load_pair(dst, src, 0, a)
        load_group(chi_sb, chi, 1)
        load_group(phi_sb, phi, 1)
        load_vector(w_sb, w)
        load_group(psi_sb, psi, 0)
        for a in range(2):
            load_pair(vker_sb, vker, 0, a)
        load_vector(dv_sb, dv)
        load_group(psi_sb, psi, 1)
        for a in range(2):
            load_pair(vker_sb, vker, 1, a)

        for g in range(GROUPS):
            for name, src in (("chi", chi_sb), ("phi", phi_sb)):
                for a in range(2):
                    turn_input(name, src, g, a)
            for a in range(2):
                make_c(g, a)
            for a in range(2):
                words_out(phi_t[:, pair_cols(g, a), :], banks["phi", g, a])
            for a in range(2):
                quantize_c(g, a)
            if g == GROUPS - 1:
                for t in range(PACK):
                    nc.vector.tensor_scalar(
                        out=g_rows[:, 0, t, :], in0=psi_sb[:, 0, t, :], scalar1=w_sb[:, 0, t : t + 1],
                        scalar2=None, op0=MULT,
                    )
            for a in range(2):
                quantize_phi(g, a)

        for t in range(PACK):
            nc.gpsimd.tensor_scalar(
                out=g_rows[:, 1, t, :], in0=psi_sb[:, 1, t, :], scalar1=w_sb[:, 1, t : t + 1],
                scalar2=0.0, op0=MULT, op1=ADD,
            )
        interleave_g(0)
        nc.scalar.activation(out=dv_f32[:], in_=dv_sb[:, :, 0:PACK], func=COPY)
        for t in range(PACK):
            make_dv_psi(0, t)
        make_dv_psi(1, 0)
        interleave_g(1)

        first = [(0, t, h) for h in range(GROUPS) for t in range(PACK)]
        for tile in first:
            dp_tile(*tile)
        for t in range(PACK - 1):
            make_m(*first[2 * t])
            make_m(*first[2 * t + 1])
            dp_tile(1, t, 0)
            dp_tile(1, t, 1)
        make_m(*first[-2])
        make_m(*first[-1])
        turn_m(0)
        turn_m(1)
        make_m(1, 0, 0)
        make_m(1, 0, 1)
        turn_m(2)
        turn_m(3)
        for n in range(PACK):
            copy_m(n)
        quantize_g(0)
        make_m(1, 1, 0)
        make_m(1, 1, 1)
        dp_tile(1, 3, 0)
        dp_tile(1, 3, 1)
        quantize_g(1)
        make_m(1, 2, 0)
        make_m(1, 2, 1)
        make_dv_psi(1, 1)
        for n in range(PACK, TILES - 1):
            turn_m(n)
        for n in range(PACK, TILES - 1):
            copy_m(n)
        make_dv_psi(1, 2)
        quantize_m(0, 2)
        make_m(1, 3, 0)
        quantize_m(2, 2)
        make_m(1, 3, 1)
        quantize_m(4, 1)

        for t in range(PACK - 1):
            k_tile(0, t)
        turn_m(TILES - 1)
        k_tile(0, PACK - 1)
        copy_m(TILES - 1)
        make_dv_psi(1, 3)
        finish(0, 0)
        quantize_m(5, 1)
        finish(0, 1)
        quantize_m(6, 1)
        finish(0, 2)
        finish(0, 3)
        quantize_m(7, 1)
        for t in range(PACK):
            k_tile(1, t)
        for a in range(2):
            interleave_res(nc.scalar.copy, 0, a)
        for t in range(PACK):
            finish(1, t)

        quantize_res(0, 0)
        interleave_res(nc.scalar.copy, 1, 0)
        interleave_res(nc.vector.tensor_copy, 1, 1)
        quantize_res(0, 1)
        store_codes(0, slice(0, J))
        for a in (1, 0):
            quantize_res(1, a)
            store_codes(1, half(a))
        for quad in range(P // QUADRANT):
            queue = nc.scalar if quad < 2 else nc.sync
            queue.dma_start(
                out=out_2[:, 4 * quad : 4 * quad + 4, :].rearrange("g r m -> r g m").bitcast(I32),
                in_=res_scales[QUADRANT * quad : QUADRANT * quad + 4].bitcast(I32),
            )
